import numpy as np
import ml_dtypes


def mxq(x, axis, fmt="e4m3"):
    dtype, down = {"e4m3": (ml_dtypes.float8_e4m3fn, 7), "e5m2": (ml_dtypes.float8_e5m2, 14)}[fmt]
    v = np.moveaxis(np.asarray(x, np.float32).astype(ml_dtypes.bfloat16).astype(np.float64), axis, -1)
    blocks = v.reshape(v.shape[:-1] + (-1, 32))
    amax = np.abs(blocks).max(-1, keepdims=True)
    byte = np.maximum(np.where(amax > 0, np.frexp(amax)[1] - 1 + 127, 0) - down, 1)
    scale = np.exp2(byte - 127.0)
    codes = (blocks / scale).astype(np.float32).astype(dtype).astype(np.float64)
    return np.moveaxis((codes * scale).reshape(v.shape), -1, axis)


WIDE = False


def mx_kscale(k):
    if not WIDE:
        return np.ones(k)
    levels = np.array([10, -10, 5, -5, 0])
    if k % 512:
        return np.exp2(np.random.permutation(np.resize(levels, k // 32))).repeat(32)
    a = np.empty((k // 512, 16))
    for p in range(k // 512):
        a[p, :8] = np.random.permutation(np.resize(levels, 8))
        for g in range(8):
            far = levels[np.abs(levels - a[p, g]) >= 10]
            a[p, g + 8] = far[np.random.randint(len(far))]
    return np.exp2(a.ravel()).repeat(32)


def f64(x):
    return np.asarray(x).astype(np.float64)


def striped(idx):
    return np.tile(idx.reshape(-1, 16).T, (8, 1)).astype(np.uint16)


def unstriped(offs):
    return offs[:16].T.reshape(-1).astype(np.int64)


E2M1 = np.array([0.0, 0.5, 1.0, 1.5, 2.0, 3.0, 4.0, 6.0, -0.0, -0.5, -1.0, -1.5, -2.0, -3.0, -4.0, -6.0])


def pack_weight(w, fmt):
    k, n = w.shape
    w = f64(np.asarray(w, np.float32).astype(ml_dtypes.bfloat16)).reshape(k // 32, 32, n)
    amax = np.abs(w).max(1)
    if fmt == "e4m3":
        byte = np.frexp(amax)[1] - 1 + 127 - 7
    else:
        mant, ex = np.frexp(amax / 6.0)
        byte = np.where(mant > 0.5, ex, ex - 1) + 127
    byte = np.clip(np.where(amax > 0, byte, 1), 1, 254)
    scaled = (w * np.exp2(127.0 - byte)[:, None, :]).reshape(k, n).astype(np.float32)
    by_word = np.ascontiguousarray(scaled.reshape(k // 512, 128, 4, n).transpose(0, 1, 3, 2))
    if fmt == "e4m3":
        words = by_word.astype(ml_dtypes.float8_e4m3fn).view(np.uint8)
    else:
        c = by_word.astype(ml_dtypes.float4_e2m1fn).view(np.uint8) & 0xF
        words = (c[..., 0::2] | (c[..., 1::2] << 4)).reshape(k // 512, 128, 2 * n)
    return np.ascontiguousarray(words), np.ascontiguousarray(byte.astype(np.uint8).reshape(k // 512, 16, n))


def unpack_weight(words, scales, fmt):
    g, _, n = scales.shape
    words = np.ascontiguousarray(words).reshape(g, 128, n, -1)
    if fmt == "e4m3":
        vals = words.view(ml_dtypes.float8_e4m3fn).astype(np.float64)
    else:
        nib = np.empty((g, 128, n, 4), np.uint8)
        nib[..., 0::2] = words & 0xF
        nib[..., 1::2] = words >> 4
        vals = E2M1[nib]
    vals = vals * np.repeat(np.exp2(scales.astype(np.float64) - 127.0), 8, axis=1)[..., None]
    return vals.transpose(0, 1, 3, 2).reshape(g * 512, n)


def gelu(v):
    return 0.5 * v * (1.0 + np.tanh(np.sqrt(2.0 / np.pi) * (v + 0.044715 * v**3)))


def striped8(idx):
    return np.concatenate([v.reshape(-1, 16).T for v in idx]).astype(np.uint16)


def unstriped8(offs):
    return np.stack([offs[16 * g:16 * g + 16].T.reshape(-1) for g in range(8)]).astype(np.int64)


def heads(h, wgt, idx8):
    r = np.arange(h.shape[0])
    return wgt[r // 4 % 128] * h[r[:, None], idx8[r % 512 // 64]]


def bf(x):
    return np.asarray(x, np.float32).astype(ml_dtypes.bfloat16)


def planes(Y):
    n, m = Y.shape
    b = f64(bf(Y)).reshape(n // 32, 32, m)
    amax = np.abs(b).max(1)
    byte = np.clip(np.where(amax > 0, np.frexp(amax)[1] - 1 + 127 - 7, 1), 1, 254)
    codes = (b * np.exp2(127.0 - byte)[:, None, :]).reshape(n, m).astype(np.float32).astype(ml_dtypes.float8_e4m3fn).view(np.uint8)
    words = codes.reshape(n // 512, 128, 4, m).transpose(0, 1, 3, 2)
    return np.ascontiguousarray(words), np.ascontiguousarray(byte.astype(np.uint8).reshape(n // 512, 16, m))


K, H, N, T, S, T2, P = 512, 1024, 512, 2048, 1024, 2048, 1024

def setup_inputs():
    n = np.random.standard_normal
    s = mx_kscale(K)[:, None]
    u = mx_kscale(H)[:, None]
    tab_words, tab_scales = pack_weight(n((K, T)) * s, "e4m3")
    w1 = n((K, H)) / np.sqrt(K) / s * u.T
    w2_words, w2_scales = pack_weight(n((K, H)) / np.sqrt(K) / s * u.T, "e2m1")
    w3_words, w3_scales = pack_weight(n((K, H)) / np.sqrt(K) / s * u.T, "e4m3")
    w4 = 0.5 * n((H, N)) / np.sqrt(H) / u * np.exp(0.8 * n(N))
    wgt = np.repeat(np.random.uniform(0.5, 2.0, (8, P)), 16, axis=0)
    tiles = np.stack([np.random.permutation(T2)[:P] for _ in range(8)])
    return {"tab_words": tab_words, "tab_scales": tab_scales,
            "w1": w1.astype(np.float32),
            "w2_words": w2_words, "w2_scales": w2_scales,
            "w3_words": w3_words, "w3_scales": w3_scales,
            "w4": w4.astype(np.float32),
            "page0": (n((H, T2)) * u).astype(np.float32),
            "pred": (1.4 * n((H, P)) * u).astype(np.float32),
            "wgs": np.exp(0.3 * n((128, S))).astype(np.float32),
            "wgt": wgt.astype(np.float32),
            "offs": striped(np.random.permutation(T)[:S]),
            "offs2": striped(np.random.permutation(T2)[:S]),
            "offs3": striped8(tiles)}

def reference(tab_words, tab_scales, w1, w2_words, w2_scales, w3_words, w3_scales, w4,
              page0, pred, wgs, wgt, offs, offs2, offs3):
    v = unpack_weight(tab_words, tab_scales, "e4m3")[:, unstriped(offs)]
    h1 = mxq(f64(w1), 0, "e4m3").T @ v
    h2 = unpack_weight(w2_words, w2_scales, "e2m1").T @ v
    h3 = unpack_weight(w3_words, w3_scales, "e4m3").T @ v
    h = np.maximum(np.maximum(h1, h2), h3)
    page = f64(page0).copy()
    page[:, unstriped(offs2)] = np.tile(f64(wgs), (H // 128, 1)) * h
    x = heads(page, f64(wgt), unstriped8(offs3))
    d = mxq(np.abs(x - f64(pred)), 0, "e4m3")
    y = mxq(f64(w4), 0, "e4m3").T @ d
    words, scales = planes(y)
    return y, words, scales

@@ -1,0 +1,312 @@
+from contextlib import ExitStack
+
+import concourse.mybir as mybir
+from concourse.masks import make_identity
+
+K, H, N, T, S, T2, M = 512, 1024, 512, 2048, 1024, 2048, 1024
+FLOPS = 2 * K * H * S * 3 + 2 * H * N * M
+
+F32 = mybir.dt.float32
+BF16 = mybir.dt.bfloat16
+I32 = mybir.dt.int32
+U32 = mybir.dt.uint32
+U16 = mybir.dt.uint16
+U8 = mybir.dt.uint8
+FP8X4 = mybir.dt.float8_e4m3fn_x4
+FP4X4 = mybir.dt.float4_e2m1fn_x4
+ALU = mybir.AluOpType
+ACT = mybir.ActivationFunctionType
+
+P = 128
+PACK = 4
+K_PASS = P * PACK
+BANK = 512
+LIST_ROWS = 16
+HX_SLOTS = 3
+TAIL = (256, 256, 256, 128, 128)
+
+
+def tile_list_drogue_deviation_features_kernel(
+    tc, tab_words, tab_scales, w1, w2_words, w2_scales, w3_words, w3_scales, w4,
+    page0, pred, wgs, wgt, offs, offs2, offs3, out_0, out_1, out_2,
+):
+    nc = tc.nc
+    passes = H // K_PASS
+
+    with ExitStack() as ctx:
+        keep = ctx.enter_context(tc.tile_pool(name="keep", bufs=1))
+        ring = ctx.enter_context(tc.tile_pool(name="ring", bufs=2))
+        psum = ctx.enter_context(tc.psum_pool(name="psum", bufs=1))
+
+        pick = keep.tile([P, S // LIST_ROWS], U16)
+        place = keep.tile([P, S // LIST_ROWS], U16)
+        collect = keep.tile([P, M // LIST_ROWS], U16)
+        tab_w = keep.tile([P, T], U32, name="pred0")
+        tab_s = keep.tile([P, T], U8, name="wgs_rest")
+        w2_raw = keep.tile([P, 2 * H], U8, name="wgs_first")
+        w3_raw = keep.tile([P, H], I32, name="page0", align_bytes=64)
+        s23_raw = keep.tile([P, H], U8, name="v_s1", align_bytes=64)
+        v_w = keep.tile([P, S], U32, align_bytes=64)
+        w2_w = keep.tile([P, 2 * H], U8, align_bytes=64)
+        w3_w = keep.tile([P, H], I32, align_bytes=64)
+        s23 = keep.tile([P, H], U8, align_bytes=64)
+        w1_w = keep.tile([P, H], U32, align_bytes=64)
+        w1_s = keep.tile([P, H], U8, align_bytes=64)
+        w4_w = keep.tile([P, passes * N], U32, align_bytes=64)
+        w4_s = keep.tile([P, passes * N], U8, align_bytes=64)
+        d_w = keep.tile([P, passes * M], U32, align_bytes=64)
+        d_s = keep.tile([P, passes * M], U8, align_bytes=64)
+        y_w = keep.tile([P, M], U32, align_bytes=64)
+        y_s = keep.tile([P, M], U8, align_bytes=64)
+        wgt_neg = keep.tile([P, M], F32)
+        ident = keep.tile([P, P], F32)
+        ident_bf = keep.tile([P, P], BF16)
+
+        def load_scale_rows(queue, plane, first_row, scales):
+            for q in range(4):
+                rows = slice(32 * q + first_row, 32 * q + first_row + 4)
+                queue.dma_start(
+                    out=plane[rows, :].bitcast(I32), in_=scales[0, 4 * q : 4 * q + 4, :].bitcast(I32)
+                )
+
+        def load_weight(rows):
+            raw = keep.tile([P, PACK, K_PASS], F32, name="w_raw")
+            nc.sync.dma_start(out=raw[:], in_=rows.rearrange("(p j) c -> p j c", j=PACK))
+            return raw
+
+        def quantize_weight(raw, codes, scales, tag):
+            grouped = keep.tile([P, K_PASS * PACK], BF16, name=tag, align_bytes=64)
+            nc.scalar.copy(
+                out=grouped[:].rearrange("p (t m j) -> p m t j", t=PACK, j=PACK),
+                in_=raw[:].rearrange("p j (m t) -> p m t j", t=PACK),
+            )
+            nc.vector.quantize_mx(out=codes.bitcast(FP8X4), scales=scales, in_=grouped[:])
+
+        def load_rows(source, b, i, name):
+            rows = keep.tile([P, source.shape[1]], F32, name=name, align_bytes=64)
+            view = source[b * K_PASS : (b + 1) * K_PASS, :].rearrange("(p i) c -> p i c", i=PACK)
+            nc.sync.dma_start(out=rows[:], in_=view[:, i, :])
+            return rows
+
+        nc.vector.memset(tab_s[:].bitcast(I32), 0)
+        nc.vector.memset(s23_raw[:].bitcast(I32), 0)
+        load_scale_rows(nc.gpsimd, s23_raw, 4, w3_scales)
+        make_identity(nc, ident[:])
+        make_identity(nc, ident_bf[:])
+        nc.sync.dma_start(
+            out=w3_raw[:], in_=w3_words[0].rearrange("p c i -> p (c i)").bitcast(I32)
+        )
+        nc.sync.dma_start(out=w2_raw[:].bitcast(I32), in_=w2_words[0].bitcast(I32))
+        nc.sync.dma_start(
+            out=tab_w[:].bitcast(I32), in_=tab_words[0].rearrange("p c i -> p (c i)").bitcast(I32)
+        )
+        nc.sync.dma_start(pick[:], offs)
+        nc.sync.dma_start(place[:], offs2)
+        nc.sync.dma_start(collect[:], offs3)
+        w1_raw = load_weight(w1[:, 0:K_PASS])
+        load_scale_rows(nc.sync, tab_s, 0, tab_scales)
+        load_scale_rows(nc.sync, s23_raw, 0, w2_scales)
+
+        nc.vector.tensor_copy(
+            out=w3_w[:].rearrange("p (b t c q) -> p b c t q", b=passes, t=PACK, q=4),
+            in_=w3_raw[:].rearrange("p (b c q t) -> p b c t q", b=passes, t=PACK, q=4),
+        )
+        nc.vector.tensor_copy(
+            out=w2_w[:].rearrange("p (b t m e) -> p b t m e", b=passes, t=PACK, e=2),
+            in_=w2_raw[:].rearrange("p (b m t e) -> p b t m e", b=passes, t=PACK, e=2),
+        )
+        halves = [slice(half * BANK, (half + 1) * BANK) for half in range(S // BANK)]
+
+        def entries_of(offsets, cols):
+            return offsets[:, cols.start // LIST_ROWS : cols.stop // LIST_ROWS]
+
+        for cols in halves:
+            nc.vector.tensor_copy(v_w[:, cols], tab_w[:].indirect(entries_of(pick, cols)))
+        v_s = [keep.tile([P, BANK], U8, name="v_s0", align_bytes=64)]
+        nc.vector.tensor_copy(v_s[0][:], tab_s[:].indirect(entries_of(pick, halves[0])))
+        nc.vector.tensor_copy(
+            out=s23[:].rearrange("p (b t m) -> p b t m", b=passes, t=PACK),
+            in_=s23_raw[:].rearrange("p (b m t) -> p b t m", b=passes, t=PACK),
+        )
+        quantize_weight(w1_raw, w1_w[:, 0:K_PASS], w1_s[:, 0:K_PASS], "page1")
+        v_s.append(keep.tile([P, BANK], U8, name="v_s1", align_bytes=64))
+        nc.vector.tensor_copy(v_s[1][:], tab_s[:].indirect(entries_of(pick, halves[1])))
+        pages = {0: load_rows(page0, 0, 0, "page0")}
+        wgs_rows = wgs.rearrange("(q i) j -> q i j", i=PACK)
+        wgs_first = keep.tile([P, S], F32, name="wgs_first")
+        wgs_rest = keep.tile([P, PACK - 1, S], F32, name="wgs_rest")
+        for q in range(4):
+            nc.sync.dma_start(out=wgs_first[32 * q : 32 * q + 32, :], in_=wgs_rows[:, 0, :])
+        pages[1] = load_rows(page0, 0, 1, "page1")
+        for q in range(4):
+            nc.sync.dma_start(out=wgs_rest[32 * q : 32 * q + 32, :, :], in_=wgs_rows[:, 1:PACK, :])
+        wgs_of = [wgs_first[:]] + [wgs_rest[:, i, :] for i in range(PACK - 1)]
+
+        def responses(s, h, half):
+            rows = slice(s * P, (s + 1) * P)
+            cols = halves[half]
+            moving = dict(rhs=v_w[:, cols].bitcast(FP8X4), rhs_scale=v_s[half][:], start=True, stop=True)
+            h3 = psum.tile([P, BANK], F32, name="h3")
+            nc.tensor.matmul_mx(
+                out=h3[:], lhsT=w3_w[:, rows].bitcast(FP8X4), lhsT_scale=s23[4:P, rows], **moving
+            )
+            h2 = psum.tile([P, BANK], F32, name="h2", bufs=2)
+            nc.tensor.matmul_mx(
+                out=h2[:], lhsT=w2_w[:, 2 * s * P : 2 * (s + 1) * P].bitcast(FP4X4),
+                lhsT_scale=s23[:, rows], **moving
+            )
+            h1 = psum.tile([P, BANK], F32, name="h1", bufs=2)
+            nc.tensor.matmul_mx(
+                out=h1[:], lhsT=w1_w[:, rows].bitcast(FP8X4), lhsT_scale=w1_s[:, rows], **moving
+            )
+            nc.scalar.copy(out=h[:, cols], in_=h3[:])
+            return h2, h1
+
+        def take_max(h, half, other):
+            nc.vector.tensor_tensor(h[:, halves[half]], other[:], h[:, halves[half]], ALU.max)
+
+        def deviations_by_transposes(i, x, pred_rows, grouped):
+            blocks = BANK // P
+            d_turned = keep.tile([P, M], BF16, name="d_turned")
+            for cols in halves:
+                turned = psum.tile([P, BANK], F32, name="turned", bufs=2)
+                for n, source in enumerate((pred_rows, x[:])):
+                    for mb in range(blocks):
+                        nc.tensor.matmul(
+                            turned[:, mb * P : (mb + 1) * P],
+                            source[:, cols.start + mb * P : cols.start + (mb + 1) * P], ident[:],
+                            is_transpose=True, start=(n == 0 and mb == 0), stop=(n == 1 and mb == blocks - 1),
+                        )
+                nc.scalar.activation(out=d_turned[:, cols], in_=turned[:], func=ACT.Abs)
+            back = psum.tile([P, M], BF16, name="back")
+            for mb in range(M // P):
+                block = slice(mb * P, (mb + 1) * P)
+                nc.tensor.transpose(back[:, block], d_turned[:, block], ident_bf[:])
+            for cols in halves:
+                nc.scalar.copy(out=grouped[:].rearrange("p (m i) -> p m i", i=PACK)[:, cols, i], in_=back[:, cols])
+
+        def quantize_d(b, cols, grouped):
+            codes = slice(b * M + cols.start, b * M + cols.stop)
+            nc.vector.quantize_mx(
+                out=d_w[:, codes].bitcast(FP8X4), scales=d_s[:, codes],
+                in_=grouped[:, PACK * cols.start : PACK * cols.stop],
+            )
+
+        def features_pass(b, cols, accs):
+            width = cols.stop - cols.start
+            per_bank = BANK // width
+            d_cols = slice(b * M + cols.start, b * M + cols.stop)
+            for t in range(PACK):
+                e = t % per_bank
+                w_cols = slice(b * N + t * P, b * N + (t + 1) * P)
+                nc.tensor.matmul_mx(
+                    out=accs[t // per_bank][:, e * width : (e + 1) * width],
+                    lhsT=w4_w[:, w_cols].bitcast(FP8X4), lhsT_scale=w4_s[:, w_cols],
+                    rhs=d_w[:, d_cols].bitcast(FP8X4), rhs_scale=d_s[:, d_cols],
+                    start=(b == 0 and e == 0), stop=(b == passes - 1 and e == per_bank - 1),
+                )
+
+        def hand_out(cols, accs):
+            width = cols.stop - cols.start
+            per_bank = BANK // width
+            y = ring.tile([P, PACK, width], F32, name="y", bufs=3)
+            for n, acc in enumerate(accs):
+                nc.scalar.copy(
+                    out=y[:, n * per_bank : (n + 1) * per_bank, :],
+                    in_=acc[:].rearrange("p (e m) -> p e m", e=per_bank),
+                )
+            nc.sync.dma_start(out=out_0.rearrange("(p t) m -> p t m", t=PACK)[:, :, cols], in_=y[:])
+            grouped = ring.tile([P, width * PACK], BF16, name="y_grouped", align_bytes=64)
+            nc.vector.tensor_copy(
+                out=grouped[:].rearrange("p (c q t) -> p c t q", q=4, t=PACK),
+                in_=y[:].rearrange("p t (c q) -> p c t q", q=4),
+            )
+            nc.vector.quantize_mx(out=y_w[:, cols].bitcast(FP8X4), scales=y_s[:, cols], in_=grouped[:])
+            words = out_1[0].rearrange("p m t -> p (m t)").bitcast(I32)
+            nc.sync.dma_start(out=words[:, cols], in_=y_w[:, cols].bitcast(I32))
+
+        def put(s, h, cols):
+            nc.vector.tensor_tensor(
+                pages[s][:].indirect(entries_of(place, cols)), h[:, cols], wgs_of[s % PACK][:, cols], ALU.mult
+            )
+
+        def load_pred(b, tag):
+            rows = keep.tile([P, PACK, M], F32, name=tag)
+            view = pred[b * K_PASS : (b + 1) * K_PASS, :].rearrange("(p i) m -> p i m", i=PACK)
+            nc.sync.dma_start(out=rows[:], in_=view)
+            return rows
+
+        def bring(s, x, cols):
+            nc.vector.tensor_tensor(
+                x[:, cols], pages[s][:].indirect(entries_of(collect, cols)), wgt_neg[:, cols], ALU.mult
+            )
+
+        whole = slice(0, S)
+        slices = passes * PACK
+        last = slices - 1
+        h = keep.tile([P, S], F32, name="h_first")
+        for half in range(len(halves)):
+            for other in responses(0, h, half):
+                take_max(h, half, other)
+            put(0, h, halves[half])
+        wgt_sb = keep.tile([P, M], F32, name="h_first")
+        nc.sync.dma_start(out=wgt_sb[:], in_=wgt)
+        nc.scalar.mul(wgt_neg[:], wgt_sb[:], -1.0)
+        preds = [load_pred(0, "pred0")]
+        xs = {}
+        grouped = None
+        for s in range(slices):
+            if s > 0:
+                put(s, h, whole)
+            if s < last:
+                h = keep.tile([P, S], F32, name="hx%d" % ((s + 1) % HX_SLOTS))
+                sums = [responses(s + 1, h, half) for half in range(len(halves))]
+                for which in range(2):
+                    for half in range(len(halves)):
+                        take_max(h, half, sums[half][which])
+                xs[s] = keep.tile([P, M], F32, name="hx%d" % (s % HX_SLOTS))
+                bring(s, xs[s], whole)
+            if s + 2 < slices:
+                pages[s + 2] = load_rows(page0, (s + 2) // PACK, (s + 2) % PACK, "page%d" % (s % 2))
+            if s == 0:
+                w1_raw = load_weight(w1[:, K_PASS : 2 * K_PASS])
+                quantize_weight(w1_raw, w1_w[:, K_PASS:H], w1_s[:, K_PASS:H], "w_grouped")
+            elif s <= passes:
+                b = s - 1
+                w4_raw = load_weight(w4[b * K_PASS : (b + 1) * K_PASS, :])
+                quantize_weight(w4_raw, w4_w[:, b * N : (b + 1) * N], w4_s[:, b * N : (b + 1) * N], "w_grouped")
+            elif s == passes + 1:
+                preds.append(load_pred(1, "w_raw"))
+            if s > 0:
+                b, i = divmod(s - 1, PACK)
+                if i == 0:
+                    grouped = ring.tile([P, M * PACK], BF16, name="d_grouped", align_bytes=64)
+                deviations_by_transposes(i, xs[s - 1], preds[b][:, i, :], grouped)
+                if i == PACK - 1:
+                    quantize_d(b, whole, grouped)
+        pred_rows = preds[passes - 1][:, PACK - 1, :]
+        pieces = [slice(sum(TAIL[:c]), sum(TAIL[: c + 1])) for c in range(len(TAIL))]
+        banks = [("h2", 2)] * 2 + [("h1", 2)] * 2 + [("h3", 1), ("turned", 2), ("turned", 2), ("back", 1)]
+        accs = []
+        for cols in pieces:
+            taken = sum(len(a) for a in accs)
+            count = PACK * (cols.stop - cols.start) // BANK
+            accs.append(
+                [psum.tile([P, BANK], F32, name=tag, bufs=bufs) for tag, bufs in banks[taken : taken + count]]
+            )
+            features_pass(0, cols, accs[-1])
+        x = keep.tile([P, M], F32, name="hx%d" % (last % HX_SLOTS))
+        for c, cols in enumerate(pieces):
+            bring(last, x, cols)
+            nc.vector.tensor_tensor(x[:, cols], x[:, cols], pred_rows[:, cols], ALU.add)
+            nc.scalar.activation(
+                out=grouped[:].rearrange("p (m i) -> p m i", i=PACK)[:, cols, PACK - 1], in_=x[:, cols], func=ACT.Abs
+            )
+            quantize_d(passes - 1, cols, grouped)
+            features_pass(passes - 1, cols, accs[c])
+        for c, cols in enumerate(pieces):
+            hand_out(cols, accs[c])
+        for q in range(4):
+            nc.sync.dma_start(
+                out=out_2[0, 4 * q : 4 * q + 4, :].bitcast(I32), in_=y_s[32 * q : 32 * q + 4, :].bitcast(I32)
+            )

@@ -69,18 +69,23 @@ def tile_list_drogue_deviation_features_kernel(
                     out=plane[rows, :].bitcast(I32), in_=scales[0, 4 * q : 4 * q + 4, :].bitcast(I32)
                 )
 
-        def load_weight(rows):
+        def load_weight(queue, rows):
             raw = keep.tile([P, PACK, K_PASS], F32, name="w_raw")
-            nc.sync.dma_start(out=raw[:], in_=rows.rearrange("(p j) c -> p j c", j=PACK))
+            queue.dma_start(out=raw[:], in_=rows.rearrange("(p j) c -> p j c", j=PACK))
             return raw
 
-        def quantize_weight(raw, codes, scales, tag):
+        def quantize_weight(raw, codes, scales, tag, parts):
             grouped = keep.tile([P, K_PASS * PACK], BF16, name=tag, align_bytes=64)
-            nc.scalar.copy(
-                out=grouped[:].rearrange("p (t m j) -> p m t j", t=PACK, j=PACK),
-                in_=raw[:].rearrange("p j (m t) -> p m t j", t=PACK),
-            )
-            nc.vector.quantize_mx(out=codes.bitcast(FP8X4), scales=scales, in_=grouped[:])
+            for part in parts:
+                nc.scalar.copy(
+                    out=grouped[:].rearrange("p (t m j) -> p m t j", t=PACK, j=PACK)[:, :, part, :],
+                    in_=raw[:].rearrange("p j (m t) -> p m t j", t=PACK)[:, :, part, :],
+                )
+                cols = slice(part.start * P, part.stop * P)
+                nc.vector.quantize_mx(
+                    out=codes[:, cols].bitcast(FP8X4), scales=scales[:, cols],
+                    in_=grouped[:, PACK * cols.start : PACK * cols.stop],
+                )
 
         def load_rows(source, b, i, name):
             rows = keep.tile([P, source.shape[1]], F32, name=name, align_bytes=64)
@@ -88,8 +93,8 @@ def tile_list_drogue_deviation_features_kernel(
             nc.sync.dma_start(out=rows[:], in_=view[:, i, :])
             return rows
 
-        nc.vector.memset(tab_s[:].bitcast(I32), 0)
-        nc.vector.memset(s23_raw[:].bitcast(I32), 0)
+        nc.gpsimd.memset(tab_s[:].bitcast(I32), 0)
+        nc.gpsimd.memset(s23_raw[:].bitcast(I32), 0)
         load_scale_rows(nc.gpsimd, s23_raw, 4, w3_scales)
         make_identity(nc, ident[:])
         make_identity(nc, ident_bf[:])
@@ -101,11 +106,11 @@ def tile_list_drogue_deviation_features_kernel(
             out=tab_w[:].bitcast(I32), in_=tab_words[0].rearrange("p c i -> p (c i)").bitcast(I32)
         )
         nc.sync.dma_start(pick[:], offs)
-        nc.sync.dma_start(place[:], offs2)
-        nc.sync.dma_start(collect[:], offs3)
-        w1_raw = load_weight(w1[:, 0:K_PASS])
         load_scale_rows(nc.sync, tab_s, 0, tab_scales)
         load_scale_rows(nc.sync, s23_raw, 0, w2_scales)
+        nc.sync.dma_start(place[:], offs2)
+        nc.sync.dma_start(collect[:], offs3)
+        w1_raw = load_weight(nc.sync, w1[:, 0:K_PASS])
 
         nc.vector.tensor_copy(
             out=w3_w[:].rearrange("p (b t c q) -> p b c t q", b=passes, t=PACK, q=4),
@@ -128,7 +133,7 @@ def tile_list_drogue_deviation_features_kernel(
             out=s23[:].rearrange("p (b t m) -> p b t m", b=passes, t=PACK),
             in_=s23_raw[:].rearrange("p (b m t) -> p b t m", b=passes, t=PACK),
         )
-        quantize_weight(w1_raw, w1_w[:, 0:K_PASS], w1_s[:, 0:K_PASS], "page1")
+        quantize_weight(w1_raw, w1_w[:, 0:K_PASS], w1_s[:, 0:K_PASS], "page1", (slice(0, 1), slice(1, PACK)))
         v_s.append(keep.tile([P, BANK], U8, name="v_s1", align_bytes=64))
         nc.vector.tensor_copy(v_s[1][:], tab_s[:].indirect(entries_of(pick, halves[1])))
         pages = {0: load_rows(page0, 0, 0, "page0")}
@@ -146,7 +151,7 @@ def tile_list_drogue_deviation_features_kernel(
             rows = slice(s * P, (s + 1) * P)
             cols = halves[half]
             moving = dict(rhs=v_w[:, cols].bitcast(FP8X4), rhs_scale=v_s[half][:], start=True, stop=True)
-            h3 = psum.tile([P, BANK], F32, name="h3")
+            h3 = psum.tile([P, BANK], F32, name="shared%d" % half)
             nc.tensor.matmul_mx(
                 out=h3[:], lhsT=w3_w[:, rows].bitcast(FP8X4), lhsT_scale=s23[4:P, rows], **moving
             )
@@ -168,8 +173,8 @@ def tile_list_drogue_deviation_features_kernel(
         def deviations_by_transposes(i, x, pred_rows, grouped):
             blocks = BANK // P
             d_turned = keep.tile([P, M], BF16, name="d_turned")
-            for cols in halves:
-                turned = psum.tile([P, BANK], F32, name="turned", bufs=2)
+            for half, cols in enumerate(halves):
+                turned = psum.tile([P, BANK], F32, name="shared%d" % half)
                 for n, source in enumerate((pred_rows, x[:])):
                     for mb in range(blocks):
                         nc.tensor.matmul(
@@ -178,7 +183,7 @@ def tile_list_drogue_deviation_features_kernel(
                             is_transpose=True, start=(n == 0 and mb == 0), stop=(n == 1 and mb == blocks - 1),
                         )
                 nc.scalar.activation(out=d_turned[:, cols], in_=turned[:], func=ACT.Abs)
-            back = psum.tile([P, M], BF16, name="back")
+            back = psum.tile([P, M], BF16, name="back", bufs=2)
             for mb in range(M // P):
                 block = slice(mb * P, (mb + 1) * P)
                 nc.tensor.transpose(back[:, block], d_turned[:, block], ident_bf[:])
@@ -230,10 +235,10 @@ def tile_list_drogue_deviation_features_kernel(
                 pages[s][:].indirect(entries_of(place, cols)), h[:, cols], wgs_of[s % PACK][:, cols], ALU.mult
             )
 
-        def load_pred(b, tag):
+        def load_pred(queue, b, tag):
             rows = keep.tile([P, PACK, M], F32, name=tag)
             view = pred[b * K_PASS : (b + 1) * K_PASS, :].rearrange("(p i) m -> p i m", i=PACK)
-            nc.sync.dma_start(out=rows[:], in_=view)
+            queue.dma_start(out=rows[:], in_=view)
             return rows
 
         def bring(s, x, cols):
@@ -241,18 +246,26 @@ def tile_list_drogue_deviation_features_kernel(
                 x[:, cols], pages[s][:].indirect(entries_of(collect, cols)), wgt_neg[:, cols], ALU.mult
             )
 
+        def difference(s, x, cols):
+            nc.vector.tensor_tensor(x[:, cols], x[:, cols], preds[s // PACK][:, s % PACK, cols], ALU.add)
+
+        def absolute(s, x, cols):
+            nc.scalar.activation(
+                out=grouped[:].rearrange("p (m i) -> p m i", i=PACK)[:, cols, s % PACK], in_=x[:, cols], func=ACT.Abs
+            )
+
         whole = slice(0, S)
         slices = passes * PACK
         last = slices - 1
-        h = keep.tile([P, S], F32, name="h_first")
+        h = keep.tile([P, S], F32, name="h_first", align_bytes=64)
         for half in range(len(halves)):
             for other in responses(0, h, half):
                 take_max(h, half, other)
             put(0, h, halves[half])
-        wgt_sb = keep.tile([P, M], F32, name="h_first")
+        wgt_sb = keep.tile([P, M], F32, name="h_first", align_bytes=64)
         nc.sync.dma_start(out=wgt_sb[:], in_=wgt)
         nc.scalar.mul(wgt_neg[:], wgt_sb[:], -1.0)
-        preds = [load_pred(0, "pred0")]
+        preds = [load_pred(nc.sync, 0, "pred0")]
         xs = {}
         grouped = None
         for s in range(slices):
@@ -269,24 +282,27 @@ def tile_list_drogue_deviation_features_kernel(
             if s + 2 < slices:
                 pages[s + 2] = load_rows(page0, (s + 2) // PACK, (s + 2) % PACK, "page%d" % (s % 2))
             if s == 0:
-                w1_raw = load_weight(w1[:, K_PASS : 2 * K_PASS])
-                quantize_weight(w1_raw, w1_w[:, K_PASS:H], w1_s[:, K_PASS:H], "w_grouped")
+                w1_raw = load_weight(nc.scalar, w1[:, K_PASS : 2 * K_PASS])
+                quantize_weight(w1_raw, w1_w[:, K_PASS:H], w1_s[:, K_PASS:H], "h_first", (slice(0, PACK),))
             elif s <= passes:
                 b = s - 1
-                w4_raw = load_weight(w4[b * K_PASS : (b + 1) * K_PASS, :])
-                quantize_weight(w4_raw, w4_w[:, b * N : (b + 1) * N], w4_s[:, b * N : (b + 1) * N], "w_grouped")
+                w4_raw = load_weight(nc.scalar, w4[b * K_PASS : (b + 1) * K_PASS, :])
+                quantize_weight(w4_raw, w4_w[:, b * N : (b + 1) * N], w4_s[:, b * N : (b + 1) * N], "h_first", (slice(0, PACK),))
             elif s == passes + 1:
-                preds.append(load_pred(1, "w_raw"))
-            if s > 0:
+                preds.append(load_pred(nc.scalar, 1, "w_raw"))
+            if s == last - 1:
+                difference(s, xs[s], whole)
+            if 0 < s < last:
                 b, i = divmod(s - 1, PACK)
                 if i == 0:
                     grouped = ring.tile([P, M * PACK], BF16, name="d_grouped", align_bytes=64)
                 deviations_by_transposes(i, xs[s - 1], preds[b][:, i, :], grouped)
                 if i == PACK - 1:
                     quantize_d(b, whole, grouped)
-        pred_rows = preds[passes - 1][:, PACK - 1, :]
+        absolute(last - 1, xs[last - 1], halves[0])
+        absolute(last - 1, xs[last - 1], halves[1])
         pieces = [slice(sum(TAIL[:c]), sum(TAIL[: c + 1])) for c in range(len(TAIL))]
-        banks = [("h2", 2)] * 2 + [("h1", 2)] * 2 + [("h3", 1), ("turned", 2), ("turned", 2), ("back", 1)]
+        banks = [("h2", 2)] * 2 + [("h1", 2)] * 2 + [("shared0", 1), ("shared1", 1)] + [("back", 2)] * 2
         accs = []
         for cols in pieces:
             taken = sum(len(a) for a in accs)
@@ -298,10 +314,8 @@ def tile_list_drogue_deviation_features_kernel(
         x = keep.tile([P, M], F32, name="hx%d" % (last % HX_SLOTS))
         for c, cols in enumerate(pieces):
             bring(last, x, cols)
-            nc.vector.tensor_tensor(x[:, cols], x[:, cols], pred_rows[:, cols], ALU.add)
-            nc.scalar.activation(
-                out=grouped[:].rearrange("p (m i) -> p m i", i=PACK)[:, cols, PACK - 1], in_=x[:, cols], func=ACT.Abs
-            )
+            difference(last, x, cols)
+            absolute(last, x, cols)
             quantize_d(passes - 1, cols, grouped)
             features_pass(passes - 1, cols, accs[c])
         for c, cols in enumerate(pieces):

@@ -45,7 +45,8 @@ def tile_list_drogue_deviation_features_kernel(
         tab_s = keep.tile([P, T], U8, name="wgs_rest")
         w2_raw = keep.tile([P, 2 * H], U8, name="wgs_first")
         w3_raw = keep.tile([P, H], I32, name="page0", align_bytes=64)
-        s23_raw = keep.tile([P, H], U8, name="v_s1", align_bytes=64)
+        s23_raw = keep.tile([P, H], U8)
+        v_s = keep.tile([P, S], U8, align_bytes=64)
         v_w = keep.tile([P, S], U32, align_bytes=64)
         w2_w = keep.tile([P, 2 * H], U8, align_bytes=64)
         w3_w = keep.tile([P, H], I32, align_bytes=64)
@@ -62,10 +63,10 @@ def tile_list_drogue_deviation_features_kernel(
         ident = keep.tile([P, P], F32)
         ident_bf = keep.tile([P, P], BF16)
 
-        def load_scale_rows(queue, plane, first_row, scales):
+        def load_scale_rows(plane, first_row, scales):
             for q in range(4):
                 rows = slice(32 * q + first_row, 32 * q + first_row + 4)
-                queue.dma_start(
+                nc.sync.dma_start(
                     out=plane[rows, :].bitcast(I32), in_=scales[0, 4 * q : 4 * q + 4, :].bitcast(I32)
                 )
 
@@ -95,9 +96,11 @@ def tile_list_drogue_deviation_features_kernel(
 
         nc.gpsimd.memset(tab_s[:].bitcast(I32), 0)
         nc.gpsimd.memset(s23_raw[:].bitcast(I32), 0)
-        load_scale_rows(nc.gpsimd, s23_raw, 4, w3_scales)
         make_identity(nc, ident[:])
         make_identity(nc, ident_bf[:])
+        nc.sync.dma_start(pick[:], offs)
+        nc.sync.dma_start(place[:], offs2)
+        nc.sync.dma_start(collect[:], offs3)
         nc.sync.dma_start(
             out=w3_raw[:], in_=w3_words[0].rearrange("p c i -> p (c i)").bitcast(I32)
         )
@@ -105,12 +108,10 @@ def tile_list_drogue_deviation_features_kernel(
         nc.sync.dma_start(
             out=tab_w[:].bitcast(I32), in_=tab_words[0].rearrange("p c i -> p (c i)").bitcast(I32)
         )
-        nc.sync.dma_start(pick[:], offs)
-        load_scale_rows(nc.sync, tab_s, 0, tab_scales)
-        load_scale_rows(nc.sync, s23_raw, 0, w2_scales)
-        nc.sync.dma_start(place[:], offs2)
-        nc.sync.dma_start(collect[:], offs3)
+        load_scale_rows(tab_s, 0, tab_scales)
+        load_scale_rows(s23_raw, 0, w2_scales)
         w1_raw = load_weight(nc.sync, w1[:, 0:K_PASS])
+        load_scale_rows(s23_raw, 4, w3_scales)
 
         nc.vector.tensor_copy(
             out=w3_w[:].rearrange("p (b t c q) -> p b c t q", b=passes, t=PACK, q=4),
@@ -127,15 +128,13 @@ def tile_list_drogue_deviation_features_kernel(
 
         for cols in halves:
             nc.vector.tensor_copy(v_w[:, cols], tab_w[:].indirect(entries_of(pick, cols)))
-        v_s = [keep.tile([P, BANK], U8, name="v_s0", align_bytes=64)]
-        nc.vector.tensor_copy(v_s[0][:], tab_s[:].indirect(entries_of(pick, halves[0])))
+        for cols in halves:
+            nc.vector.tensor_copy(v_s[:, cols], tab_s[:].indirect(entries_of(pick, cols)))
+        quantize_weight(w1_raw, w1_w[:, 0:K_PASS], w1_s[:, 0:K_PASS], "page1", (slice(0, 1), slice(1, PACK)))
         nc.vector.tensor_copy(
             out=s23[:].rearrange("p (b t m) -> p b t m", b=passes, t=PACK),
             in_=s23_raw[:].rearrange("p (b m t) -> p b t m", b=passes, t=PACK),
         )
-        quantize_weight(w1_raw, w1_w[:, 0:K_PASS], w1_s[:, 0:K_PASS], "page1", (slice(0, 1), slice(1, PACK)))
-        v_s.append(keep.tile([P, BANK], U8, name="v_s1", align_bytes=64))
-        nc.vector.tensor_copy(v_s[1][:], tab_s[:].indirect(entries_of(pick, halves[1])))
         pages = {0: load_rows(page0, 0, 0, "page0")}
         wgs_rows = wgs.rearrange("(q i) j -> q i j", i=PACK)
         wgs_first = keep.tile([P, S], F32, name="wgs_first")
@@ -150,8 +149,12 @@ def tile_list_drogue_deviation_features_kernel(
         def responses(s, h, half):
             rows = slice(s * P, (s + 1) * P)
             cols = halves[half]
-            moving = dict(rhs=v_w[:, cols].bitcast(FP8X4), rhs_scale=v_s[half][:], start=True, stop=True)
-            h3 = psum.tile([P, BANK], F32, name="shared%d" % half)
+            moving = dict(rhs=v_w[:, cols].bitcast(FP8X4), rhs_scale=v_s[:, cols], start=True, stop=True)
+            h1 = psum.tile([P, BANK], F32, name="shared%d" % half)
+            nc.tensor.matmul_mx(
+                out=h1[:], lhsT=w1_w[:, rows].bitcast(FP8X4), lhsT_scale=w1_s[:, rows], **moving
+            )
+            h3 = psum.tile([P, BANK], F32, name="h3", bufs=2)
             nc.tensor.matmul_mx(
                 out=h3[:], lhsT=w3_w[:, rows].bitcast(FP8X4), lhsT_scale=s23[4:P, rows], **moving
             )
@@ -160,12 +163,8 @@ def tile_list_drogue_deviation_features_kernel(
                 out=h2[:], lhsT=w2_w[:, 2 * s * P : 2 * (s + 1) * P].bitcast(FP4X4),
                 lhsT_scale=s23[:, rows], **moving
             )
-            h1 = psum.tile([P, BANK], F32, name="h1", bufs=2)
-            nc.tensor.matmul_mx(
-                out=h1[:], lhsT=w1_w[:, rows].bitcast(FP8X4), lhsT_scale=w1_s[:, rows], **moving
-            )
-            nc.scalar.copy(out=h[:, cols], in_=h3[:])
-            return h2, h1
+            nc.scalar.copy(out=h[:, cols], in_=h1[:])
+            return h3, h2
 
         def take_max(h, half, other):
             nc.vector.tensor_tensor(h[:, halves[half]], other[:], h[:, halves[half]], ALU.max)
@@ -214,14 +213,14 @@ def tile_list_drogue_deviation_features_kernel(
         def hand_out(cols, accs):
             width = cols.stop - cols.start
             per_bank = BANK // width
-            y = ring.tile([P, PACK, width], F32, name="y", bufs=3)
+            y = ring.tile([P, PACK, width], F32, name="y", bufs=len(TAIL))
             for n, acc in enumerate(accs):
                 nc.scalar.copy(
                     out=y[:, n * per_bank : (n + 1) * per_bank, :],
                     in_=acc[:].rearrange("p (e m) -> p e m", e=per_bank),
                 )
             nc.sync.dma_start(out=out_0.rearrange("(p t) m -> p t m", t=PACK)[:, :, cols], in_=y[:])
-            grouped = ring.tile([P, width * PACK], BF16, name="y_grouped", align_bytes=64)
+            grouped = ring.tile([P, width * PACK], BF16, name="y_grouped", bufs=len(TAIL), align_bytes=64)
             nc.vector.tensor_copy(
                 out=grouped[:].rearrange("p (c q t) -> p c t q", q=4, t=PACK),
                 in_=y[:].rearrange("p t (c q) -> p c t q", q=4),
@@ -302,7 +301,7 @@ def tile_list_drogue_deviation_features_kernel(
         absolute(last - 1, xs[last - 1], halves[0])
         absolute(last - 1, xs[last - 1], halves[1])
         pieces = [slice(sum(TAIL[:c]), sum(TAIL[: c + 1])) for c in range(len(TAIL))]
-        banks = [("h2", 2)] * 2 + [("h1", 2)] * 2 + [("shared0", 1), ("shared1", 1)] + [("back", 2)] * 2
+        banks = [("h3", 2)] * 2 + [("h2", 2)] * 2 + [("shared0", 1), ("shared1", 1)] + [("back", 2)] * 2
         accs = []
         for cols in pieces:
             taken = sum(len(a) for a in accs)

@@ -22,7 +22,7 @@ PACK = 4
 K_PASS = P * PACK
 BANK = 512
 LIST_ROWS = 16
-HX_SLOTS = 3
+PAGES = 3
 TAIL = (256, 256, 256, 128, 128)
 
 
@@ -45,7 +45,7 @@ def tile_list_drogue_deviation_features_kernel(
         tab_s = keep.tile([P, T], U8, name="wgs_rest")
         w2_raw = keep.tile([P, 2 * H], U8, name="wgs_first")
         w3_raw = keep.tile([P, H], I32, name="page0", align_bytes=64)
-        s23_raw = keep.tile([P, H], U8)
+        s23_raw = keep.tile([P, H], U8, name="page2", align_bytes=64)
         v_s = keep.tile([P, S], U8, align_bytes=64)
         v_w = keep.tile([P, S], U32, align_bytes=64)
         w2_w = keep.tile([P, 2 * H], U8, align_bytes=64)
@@ -166,15 +166,15 @@ def tile_list_drogue_deviation_features_kernel(
             nc.scalar.copy(out=h[:, cols], in_=h1[:])
             return h3, h2
 
-        def take_max(h, half, other):
-            nc.vector.tensor_tensor(h[:, halves[half]], other[:], h[:, halves[half]], ALU.max)
+        def take_max(h, half, bank, so_far):
+            nc.vector.tensor_tensor(h[:, halves[half]], bank[:], so_far[:, halves[half]], ALU.max)
 
         def deviations_by_transposes(i, x, pred_rows, grouped):
             blocks = BANK // P
             d_turned = keep.tile([P, M], BF16, name="d_turned")
             for half, cols in enumerate(halves):
                 turned = psum.tile([P, BANK], F32, name="shared%d" % half)
-                for n, source in enumerate((pred_rows, x[:])):
+                for n, source in enumerate((pred_rows, x)):
                     for mb in range(blocks):
                         nc.tensor.matmul(
                             turned[:, mb * P : (mb + 1) * P],
@@ -245,41 +245,41 @@ def tile_list_drogue_deviation_features_kernel(
                 x[:, cols], pages[s][:].indirect(entries_of(collect, cols)), wgt_neg[:, cols], ALU.mult
             )
 
-        def difference(s, x, cols):
-            nc.vector.tensor_tensor(x[:, cols], x[:, cols], preds[s // PACK][:, s % PACK, cols], ALU.add)
-
-        def absolute(s, x, cols):
-            nc.scalar.activation(
-                out=grouped[:].rearrange("p (m i) -> p m i", i=PACK)[:, cols, s % PACK], in_=x[:, cols], func=ACT.Abs
-            )
-
         whole = slice(0, S)
         slices = passes * PACK
         last = slices - 1
         h = keep.tile([P, S], F32, name="h_first", align_bytes=64)
         for half in range(len(halves)):
             for other in responses(0, h, half):
-                take_max(h, half, other)
+                take_max(h, half, other, h)
             put(0, h, halves[half])
         wgt_sb = keep.tile([P, M], F32, name="h_first", align_bytes=64)
         nc.sync.dma_start(out=wgt_sb[:], in_=wgt)
         nc.scalar.mul(wgt_neg[:], wgt_sb[:], -1.0)
         preds = [load_pred(nc.sync, 0, "pred0")]
+        pages[2] = load_rows(page0, 0, 2, "page2")
         xs = {}
         grouped = None
         for s in range(slices):
             if s > 0:
                 put(s, h, whole)
             if s < last:
-                h = keep.tile([P, S], F32, name="hx%d" % ((s + 1) % HX_SLOTS))
-                sums = [responses(s + 1, h, half) for half in range(len(halves))]
-                for which in range(2):
+                h1 = keep.tile([P, S], F32, name="h1x%d" % (s % 2))
+                sums = [responses(s + 1, h1, half) for half in range(len(halves))]
+                h = ring.tile([P, S], F32, name="h")
+                for which, so_far in enumerate((h1, h)):
                     for half in range(len(halves)):
-                        take_max(h, half, sums[half][which])
-                xs[s] = keep.tile([P, M], F32, name="hx%d" % (s % HX_SLOTS))
+                        take_max(h, half, sums[half][which], so_far)
+                if s < last - 1:
+                    xs[s] = keep.tile([P, M], F32, name="h1x%d" % (s % 2))[:]
+                else:
+                    x_pair = keep.tile([P, 2 * M], F32, name="h1x%d" % (s % 2))
+                    xs[s], xs[last] = x_pair[:, 0:M], x_pair[:, M : 2 * M]
                 bring(s, xs[s], whole)
-            if s + 2 < slices:
-                pages[s + 2] = load_rows(page0, (s + 2) // PACK, (s + 2) % PACK, "page%d" % (s % 2))
+            if s + PAGES < slices:
+                pages[s + PAGES] = load_rows(
+                    page0, (s + PAGES) // PACK, (s + PAGES) % PACK, "page%d" % (s % PAGES)
+                )
             if s == 0:
                 w1_raw = load_weight(nc.scalar, w1[:, K_PASS : 2 * K_PASS])
                 quantize_weight(w1_raw, w1_w[:, K_PASS:H], w1_s[:, K_PASS:H], "h_first", (slice(0, PACK),))
@@ -289,8 +289,6 @@ def tile_list_drogue_deviation_features_kernel(
                 quantize_weight(w4_raw, w4_w[:, b * N : (b + 1) * N], w4_s[:, b * N : (b + 1) * N], "h_first", (slice(0, PACK),))
             elif s == passes + 1:
                 preds.append(load_pred(nc.scalar, 1, "w_raw"))
-            if s == last - 1:
-                difference(s, xs[s], whole)
             if 0 < s < last:
                 b, i = divmod(s - 1, PACK)
                 if i == 0:
@@ -298,8 +296,6 @@ def tile_list_drogue_deviation_features_kernel(
                 deviations_by_transposes(i, xs[s - 1], preds[b][:, i, :], grouped)
                 if i == PACK - 1:
                     quantize_d(b, whole, grouped)
-        absolute(last - 1, xs[last - 1], halves[0])
-        absolute(last - 1, xs[last - 1], halves[1])
         pieces = [slice(sum(TAIL[:c]), sum(TAIL[: c + 1])) for c in range(len(TAIL))]
         banks = [("h3", 2)] * 2 + [("h2", 2)] * 2 + [("shared0", 1), ("shared1", 1)] + [("back", 2)] * 2
         accs = []
@@ -310,11 +306,14 @@ def tile_list_drogue_deviation_features_kernel(
                 [psum.tile([P, BANK], F32, name=tag, bufs=bufs) for tag, bufs in banks[taken : taken + count]]
             )
             features_pass(0, cols, accs[-1])
-        x = keep.tile([P, M], F32, name="hx%d" % (last % HX_SLOTS))
         for c, cols in enumerate(pieces):
-            bring(last, x, cols)
-            difference(last, x, cols)
-            absolute(last, x, cols)
+            bring(last, xs[last], cols)
+            pair = x_pair[:].rearrange("p (e m) -> p e m", e=2)[:, :, cols]
+            nc.vector.tensor_tensor(pair, pair, preds[passes - 1][:, PACK - 2 : PACK, cols], ALU.add)
+            nc.scalar.activation(
+                out=grouped[:].rearrange("p (m i) -> p m i", i=PACK)[:, cols, PACK - 2 : PACK],
+                in_=pair.rearrange("p e m -> p m e"), func=ACT.Abs,
+            )
             quantize_d(passes - 1, cols, grouped)
             features_pass(passes - 1, cols, accs[c])
         for c, cols in enumerate(pieces):

from contextlib import ExitStack

import concourse.mybir as mybir
from concourse.masks import make_identity

K, H, N, T, S, T2, M = 512, 1024, 512, 2048, 1024, 2048, 1024
FLOPS = 2 * K * H * S * 3 + 2 * H * N * M

F32 = mybir.dt.float32
BF16 = mybir.dt.bfloat16
I32 = mybir.dt.int32
U32 = mybir.dt.uint32
U16 = mybir.dt.uint16
U8 = mybir.dt.uint8
FP8X4 = mybir.dt.float8_e4m3fn_x4
FP4X4 = mybir.dt.float4_e2m1fn_x4
ALU = mybir.AluOpType
ACT = mybir.ActivationFunctionType

P = 128
PACK = 4
K_PASS = P * PACK
BANK = 512
LIST_ROWS = 16
PAGES = 3
TAIL = (256, 256, 256, 128, 128)


def tile_list_drogue_deviation_features_kernel(
    tc, tab_words, tab_scales, w1, w2_words, w2_scales, w3_words, w3_scales, w4,
    page0, pred, wgs, wgt, offs, offs2, offs3, out_0, out_1, out_2,
):
    nc = tc.nc
    passes = H // K_PASS

    with ExitStack() as ctx:
        keep = ctx.enter_context(tc.tile_pool(name="keep", bufs=1))
        ring = ctx.enter_context(tc.tile_pool(name="ring", bufs=2))
        psum = ctx.enter_context(tc.psum_pool(name="psum", bufs=1))

        pick = keep.tile([P, S // LIST_ROWS], U16)
        place = keep.tile([P, S // LIST_ROWS], U16)
        collect = keep.tile([P, M // LIST_ROWS], U16)
        tab_w = keep.tile([P, T], U32, name="pred0")
        tab_s = keep.tile([P, T], U8, name="wgs_rest")
        w2_raw = keep.tile([P, 2 * H], U8, name="wgs_first")
        w3_raw = keep.tile([P, H], I32, name="page0", align_bytes=64)
        s23_raw = keep.tile([P, H], U8, name="page2", align_bytes=64)
        v_s = keep.tile([P, S], U8, align_bytes=64)
        v_w = keep.tile([P, S], U32, align_bytes=64)
        w2_w = keep.tile([P, 2 * H], U8, align_bytes=64)
        w3_w = keep.tile([P, H], I32, align_bytes=64)
        s23 = keep.tile([P, H], U8, align_bytes=64)
        w1_w = keep.tile([P, H], U32, align_bytes=64)
        w1_s = keep.tile([P, H], U8, align_bytes=64)
        w4_w = keep.tile([P, passes * N], U32, align_bytes=64)
        w4_s = keep.tile([P, passes * N], U8, align_bytes=64)
        d_w = keep.tile([P, passes * M], U32, align_bytes=64)
        d_s = keep.tile([P, passes * M], U8, align_bytes=64)
        y_w = keep.tile([P, M], U32, align_bytes=64)
        y_s = keep.tile([P, M], U8, align_bytes=64)
        wgt_neg = keep.tile([P, M], F32)
        ident = keep.tile([P, P], F32)
        ident_bf = keep.tile([P, P], BF16)

        def load_scale_rows(plane, first_row, scales):
            for q in range(4):
                rows = slice(32 * q + first_row, 32 * q + first_row + 4)
                nc.sync.dma_start(
                    out=plane[rows, :].bitcast(I32), in_=scales[0, 4 * q : 4 * q + 4, :].bitcast(I32)
                )

        def load_weight(queue, rows):
            raw = keep.tile([P, PACK, K_PASS], F32, name="w_raw")
            queue.dma_start(out=raw[:], in_=rows.rearrange("(p j) c -> p j c", j=PACK))
            return raw

        def quantize_weight(raw, codes, scales, tag, parts):
            grouped = keep.tile([P, K_PASS * PACK], BF16, name=tag, align_bytes=64)
            for part in parts:
                nc.scalar.copy(
                    out=grouped[:].rearrange("p (t m j) -> p m t j", t=PACK, j=PACK)[:, :, part, :],
                    in_=raw[:].rearrange("p j (m t) -> p m t j", t=PACK)[:, :, part, :],
                )
                cols = slice(part.start * P, part.stop * P)
                nc.vector.quantize_mx(
                    out=codes[:, cols].bitcast(FP8X4), scales=scales[:, cols],
                    in_=grouped[:, PACK * cols.start : PACK * cols.stop],
                )

        def load_rows(source, b, i, name):
            rows = keep.tile([P, source.shape[1]], F32, name=name, align_bytes=64)
            view = source[b * K_PASS : (b + 1) * K_PASS, :].rearrange("(p i) c -> p i c", i=PACK)
            nc.sync.dma_start(out=rows[:], in_=view[:, i, :])
            return rows

        nc.gpsimd.memset(tab_s[:].bitcast(I32), 0)
        nc.gpsimd.memset(s23_raw[:].bitcast(I32), 0)
        make_identity(nc, ident[:])
        make_identity(nc, ident_bf[:])
        nc.sync.dma_start(pick[:], offs)
        nc.sync.dma_start(place[:], offs2)
        nc.sync.dma_start(collect[:], offs3)
        nc.sync.dma_start(
            out=w3_raw[:], in_=w3_words[0].rearrange("p c i -> p (c i)").bitcast(I32)
        )
        nc.sync.dma_start(out=w2_raw[:].bitcast(I32), in_=w2_words[0].bitcast(I32))
        nc.sync.dma_start(
            out=tab_w[:].bitcast(I32), in_=tab_words[0].rearrange("p c i -> p (c i)").bitcast(I32)
        )
        load_scale_rows(tab_s, 0, tab_scales)
        load_scale_rows(s23_raw, 0, w2_scales)
        w1_raw = load_weight(nc.sync, w1[:, 0:K_PASS])
        load_scale_rows(s23_raw, 4, w3_scales)

        nc.vector.tensor_copy(
            out=w3_w[:].rearrange("p (b t c q) -> p b c t q", b=passes, t=PACK, q=4),
            in_=w3_raw[:].rearrange("p (b c q t) -> p b c t q", b=passes, t=PACK, q=4),
        )
        nc.vector.tensor_copy(
            out=w2_w[:].rearrange("p (b t m e) -> p b t m e", b=passes, t=PACK, e=2),
            in_=w2_raw[:].rearrange("p (b m t e) -> p b t m e", b=passes, t=PACK, e=2),
        )
        halves = [slice(half * BANK, (half + 1) * BANK) for half in range(S // BANK)]

        def entries_of(offsets, cols):
            return offsets[:, cols.start // LIST_ROWS : cols.stop // LIST_ROWS]

        for cols in halves:
            nc.vector.tensor_copy(v_w[:, cols], tab_w[:].indirect(entries_of(pick, cols)))
        for cols in halves:
            nc.vector.tensor_copy(v_s[:, cols], tab_s[:].indirect(entries_of(pick, cols)))
        quantize_weight(w1_raw, w1_w[:, 0:K_PASS], w1_s[:, 0:K_PASS], "page1", (slice(0, 1), slice(1, PACK)))
        nc.vector.tensor_copy(
            out=s23[:].rearrange("p (b t m) -> p b t m", b=passes, t=PACK),
            in_=s23_raw[:].rearrange("p (b m t) -> p b t m", b=passes, t=PACK),
        )
        pages = {0: load_rows(page0, 0, 0, "page0")}
        wgs_rows = wgs.rearrange("(q i) j -> q i j", i=PACK)
        wgs_first = keep.tile([P, S], F32, name="wgs_first")
        wgs_rest = keep.tile([P, PACK - 1, S], F32, name="wgs_rest")
        for q in range(4):
            nc.sync.dma_start(out=wgs_first[32 * q : 32 * q + 32, :], in_=wgs_rows[:, 0, :])
        pages[1] = load_rows(page0, 0, 1, "page1")
        for q in range(4):
            nc.sync.dma_start(out=wgs_rest[32 * q : 32 * q + 32, :, :], in_=wgs_rows[:, 1:PACK, :])
        wgs_of = [wgs_first[:]] + [wgs_rest[:, i, :] for i in range(PACK - 1)]

        def responses(s, h, half):
            rows = slice(s * P, (s + 1) * P)
            cols = halves[half]
            moving = dict(rhs=v_w[:, cols].bitcast(FP8X4), rhs_scale=v_s[:, cols], start=True, stop=True)
            h1 = psum.tile([P, BANK], F32, name="shared%d" % half)
            nc.tensor.matmul_mx(
                out=h1[:], lhsT=w1_w[:, rows].bitcast(FP8X4), lhsT_scale=w1_s[:, rows], **moving
            )
            h3 = psum.tile([P, BANK], F32, name="h3", bufs=2)
            nc.tensor.matmul_mx(
                out=h3[:], lhsT=w3_w[:, rows].bitcast(FP8X4), lhsT_scale=s23[4:P, rows], **moving
            )
            h2 = psum.tile([P, BANK], F32, name="h2", bufs=2)
            nc.tensor.matmul_mx(
                out=h2[:], lhsT=w2_w[:, 2 * s * P : 2 * (s + 1) * P].bitcast(FP4X4),
                lhsT_scale=s23[:, rows], **moving
            )
            nc.scalar.copy(out=h[:, cols], in_=h1[:])
            return h3, h2

        def take_max(h, half, bank, so_far):
            nc.vector.tensor_tensor(h[:, halves[half]], bank[:], so_far[:, halves[half]], ALU.max)

        def deviations_by_transposes(i, x, pred_rows, grouped):
            blocks = BANK // P
            d_turned = keep.tile([P, M], BF16, name="d_turned")
            for half, cols in enumerate(halves):
                turned = psum.tile([P, BANK], F32, name="shared%d" % half)
                for n, source in enumerate((pred_rows, x)):
                    for mb in range(blocks):
                        nc.tensor.matmul(
                            turned[:, mb * P : (mb + 1) * P],
                            source[:, cols.start + mb * P : cols.start + (mb + 1) * P], ident[:],
                            is_transpose=True, start=(n == 0 and mb == 0), stop=(n == 1 and mb == blocks - 1),
                        )
                nc.scalar.activation(out=d_turned[:, cols], in_=turned[:], func=ACT.Abs)
            back = psum.tile([P, M], BF16, name="back", bufs=2)
            for mb in range(M // P):
                block = slice(mb * P, (mb + 1) * P)
                nc.tensor.transpose(back[:, block], d_turned[:, block], ident_bf[:])
            for cols in halves:
                nc.scalar.copy(out=grouped[:].rearrange("p (m i) -> p m i", i=PACK)[:, cols, i], in_=back[:, cols])

        def quantize_d(b, cols, grouped):
            codes = slice(b * M + cols.start, b * M + cols.stop)
            nc.vector.quantize_mx(
                out=d_w[:, codes].bitcast(FP8X4), scales=d_s[:, codes],
                in_=grouped[:, PACK * cols.start : PACK * cols.stop],
            )

        def features_pass(b, cols, accs):
            width = cols.stop - cols.start
            per_bank = BANK // width
            d_cols = slice(b * M + cols.start, b * M + cols.stop)
            for t in range(PACK):
                e = t % per_bank
                w_cols = slice(b * N + t * P, b * N + (t + 1) * P)
                nc.tensor.matmul_mx(
                    out=accs[t // per_bank][:, e * width : (e + 1) * width],
                    lhsT=w4_w[:, w_cols].bitcast(FP8X4), lhsT_scale=w4_s[:, w_cols],
                    rhs=d_w[:, d_cols].bitcast(FP8X4), rhs_scale=d_s[:, d_cols],
                    start=(b == 0 and e == 0), stop=(b == passes - 1 and e == per_bank - 1),
                )

        def hand_out(cols, accs):
            width = cols.stop - cols.start
            per_bank = BANK // width
            y = ring.tile([P, PACK, width], F32, name="y", bufs=len(TAIL))
            for n, acc in enumerate(accs):
                nc.scalar.copy(
                    out=y[:, n * per_bank : (n + 1) * per_bank, :],
                    in_=acc[:].rearrange("p (e m) -> p e m", e=per_bank),
                )
            nc.sync.dma_start(out=out_0.rearrange("(p t) m -> p t m", t=PACK)[:, :, cols], in_=y[:])
            grouped = ring.tile([P, width * PACK], BF16, name="y_grouped", bufs=len(TAIL), align_bytes=64)
            nc.vector.tensor_copy(
                out=grouped[:].rearrange("p (c q t) -> p c t q", q=4, t=PACK),
                in_=y[:].rearrange("p t (c q) -> p c t q", q=4),
            )
            nc.vector.quantize_mx(out=y_w[:, cols].bitcast(FP8X4), scales=y_s[:, cols], in_=grouped[:])
            words = out_1[0].rearrange("p m t -> p (m t)").bitcast(I32)
            nc.sync.dma_start(out=words[:, cols], in_=y_w[:, cols].bitcast(I32))

        def put(s, h, cols):
            nc.vector.tensor_tensor(
                pages[s][:].indirect(entries_of(place, cols)), h[:, cols], wgs_of[s % PACK][:, cols], ALU.mult
            )

        def load_pred(queue, b, tag):
            rows = keep.tile([P, PACK, M], F32, name=tag)
            view = pred[b * K_PASS : (b + 1) * K_PASS, :].rearrange("(p i) m -> p i m", i=PACK)
            queue.dma_start(out=rows[:], in_=view)
            return rows

        def bring(s, x, cols):
            nc.vector.tensor_tensor(
                x[:, cols], pages[s][:].indirect(entries_of(collect, cols)), wgt_neg[:, cols], ALU.mult
            )

        whole = slice(0, S)
        slices = passes * PACK
        last = slices - 1
        h = keep.tile([P, S], F32, name="h_first", align_bytes=64)
        for half in range(len(halves)):
            for other in responses(0, h, half):
                take_max(h, half, other, h)
            put(0, h, halves[half])
        wgt_sb = keep.tile([P, M], F32, name="h_first", align_bytes=64)
        nc.sync.dma_start(out=wgt_sb[:], in_=wgt)
        nc.scalar.mul(wgt_neg[:], wgt_sb[:], -1.0)
        preds = [load_pred(nc.sync, 0, "pred0")]
        pages[2] = load_rows(page0, 0, 2, "page2")
        xs = {}
        grouped = None
        for s in range(slices):
            if s > 0:
                put(s, h, whole)
            if s < last:
                h1 = keep.tile([P, S], F32, name="h1x%d" % (s % 2))
                sums = [responses(s + 1, h1, half) for half in range(len(halves))]
                h = ring.tile([P, S], F32, name="h")
                for which, so_far in enumerate((h1, h)):
                    for half in range(len(halves)):
                        take_max(h, half, sums[half][which], so_far)
                if s < last - 1:
                    xs[s] = keep.tile([P, M], F32, name="h1x%d" % (s % 2))[:]
                else:
                    x_pair = keep.tile([P, 2 * M], F32, name="h1x%d" % (s % 2))
                    xs[s], xs[last] = x_pair[:, 0:M], x_pair[:, M : 2 * M]
                bring(s, xs[s], whole)
            if s + PAGES < slices:
                pages[s + PAGES] = load_rows(
                    page0, (s + PAGES) // PACK, (s + PAGES) % PACK, "page%d" % (s % PAGES)
                )
            if s == 0:
                w1_raw = load_weight(nc.scalar, w1[:, K_PASS : 2 * K_PASS])
                quantize_weight(w1_raw, w1_w[:, K_PASS:H], w1_s[:, K_PASS:H], "h_first", (slice(0, PACK),))
            elif s <= passes:
                b = s - 1
                w4_raw = load_weight(nc.scalar, w4[b * K_PASS : (b + 1) * K_PASS, :])
                quantize_weight(w4_raw, w4_w[:, b * N : (b + 1) * N], w4_s[:, b * N : (b + 1) * N], "h_first", (slice(0, PACK),))
            elif s == passes + 1:
                preds.append(load_pred(nc.scalar, 1, "w_raw"))
            if 0 < s < last:
                b, i = divmod(s - 1, PACK)
                if i == 0:
                    grouped = ring.tile([P, M * PACK], BF16, name="d_grouped", align_bytes=64)
                deviations_by_transposes(i, xs[s - 1], preds[b][:, i, :], grouped)
                if i == PACK - 1:
                    quantize_d(b, whole, grouped)
        pieces = [slice(sum(TAIL[:c]), sum(TAIL[: c + 1])) for c in range(len(TAIL))]
        banks = [("h3", 2)] * 2 + [("h2", 2)] * 2 + [("shared0", 1), ("shared1", 1)] + [("back", 2)] * 2
        accs = []
        for cols in pieces:
            taken = sum(len(a) for a in accs)
            count = PACK * (cols.stop - cols.start) // BANK
            accs.append(
                [psum.tile([P, BANK], F32, name=tag, bufs=bufs) for tag, bufs in banks[taken : taken + count]]
            )
            features_pass(0, cols, accs[-1])
        for c, cols in enumerate(pieces):
            bring(last, xs[last], cols)
            pair = x_pair[:].rearrange("p (e m) -> p e m", e=2)[:, :, cols]
            nc.vector.tensor_tensor(pair, pair, preds[passes - 1][:, PACK - 2 : PACK, cols], ALU.add)
            nc.scalar.activation(
                out=grouped[:].rearrange("p (m i) -> p m i", i=PACK)[:, cols, PACK - 2 : PACK],
                in_=pair.rearrange("p e m -> p m e"), func=ACT.Abs,
            )
            quantize_d(passes - 1, cols, grouped)
            features_pass(passes - 1, cols, accs[c])
        for c, cols in enumerate(pieces):
            hand_out(cols, accs[c])
        for q in range(4):
            nc.sync.dma_start(
                out=out_2[0, 4 * q : 4 * q + 4, :].bitcast(I32), in_=y_s[32 * q : 32 * q + 4, :].bitcast(I32)
            )
